import numpy as np
import ml_dtypes


def mxq(x, axis, fmt="e4m3"):
    dtype, down = {"e4m3": (ml_dtypes.float8_e4m3fn, 7), "e5m2": (ml_dtypes.float8_e5m2, 14)}[fmt]
    v = np.moveaxis(np.asarray(x, np.float32).astype(ml_dtypes.bfloat16).astype(np.float64), axis, -1)
    blocks = v.reshape(v.shape[:-1] + (-1, 32))
    amax = np.abs(blocks).max(-1, keepdims=True)
    byte = np.maximum(np.where(amax > 0, np.frexp(amax)[1] - 1 + 127, 0) - down, 1)
    scale = np.exp2(byte - 127.0)
    codes = (blocks / scale).astype(np.float32).astype(dtype).astype(np.float64)
    return np.moveaxis((codes * scale).reshape(v.shape), -1, axis)


WIDE = False


def mx_kscale(k):
    if not WIDE:
        return np.ones(k)
    levels = np.array([10, -10, 5, -5, 0])
    if k % 512:
        return np.exp2(np.random.permutation(np.resize(levels, k // 32))).repeat(32)
    a = np.empty((k // 512, 16))
    for p in range(k // 512):
        a[p, :8] = np.random.permutation(np.resize(levels, 8))
        for g in range(8):
            far = levels[np.abs(levels - a[p, g]) >= 10]
            a[p, g + 8] = far[np.random.randint(len(far))]
    return np.exp2(a.ravel()).repeat(32)


def f64(x):
    return np.asarray(x).astype(np.float64)


def striped(idx):
    return np.tile(idx.reshape(-1, 16).T, (8, 1)).astype(np.uint16)


def unstriped(offs):
    return offs[:16].T.reshape(-1).astype(np.int64)


def striped8(idx):
    return np.concatenate([x.reshape(-1, 16).T for x in idx]).astype(np.uint16)


def runs(offs, k):
    lists = np.stack([offs[16 * r : 16 * r + 16].T.reshape(-1) for r in range(8)]).astype(np.int64)
    return lists[np.arange(k) % 512 // 64]


def pack_weight(w):
    k, n = w.shape
    w = f64(np.asarray(w, np.float32).astype(ml_dtypes.bfloat16)).reshape(k // 32, 32, n)
    amax = np.abs(w).max(1)
    byte = np.clip(np.where(amax > 0, np.frexp(amax)[1] - 1 + 127 - 7, 1), 1, 254)
    scaled = (w * np.exp2(127.0 - byte)[:, None, :]).reshape(k, n).astype(np.float32)
    words = np.ascontiguousarray(scaled.reshape(k // 512, 128, 4, n).transpose(0, 1, 3, 2)).astype(ml_dtypes.float8_e4m3fn).view(np.uint8)
    return words, np.ascontiguousarray(byte.astype(np.uint8).reshape(k // 512, 16, n))


def unpack_weight(words, scales):
    g, p, n, _ = words.shape
    vals = np.ascontiguousarray(words).view(ml_dtypes.float8_e4m3fn).astype(np.float64) * np.repeat(np.exp2(scales.astype(np.float64) - 127.0), 8, axis=1)[..., None]
    return vals.transpose(0, 1, 3, 2).reshape(g * 512, n)


def sigmoid(v):
    return 1.0 / (1.0 + np.exp(-np.maximum(v, -700.0)))


K, T, S, N, H, U = 512, 2048, 512, 512, 512, 1024


def setup_inputs():
    n = np.random.standard_normal
    s = mx_kscale(K)[:, None]
    u = mx_kscale(H)
    packed_xT = pack_weight(n((K, T)) * s)
    return {
        "x_words": packed_xT[0],
        "x_scales": packed_xT[1],
        "w1": (n((K, H)) / np.sqrt(K) / s).astype(np.float32),
        "gn": (np.random.uniform(0.5, 1.5, (H, 1)) * u[:, None]).astype(np.float32),
        "w2": (n((H, N)) / np.sqrt(H) / u[:, None]).astype(np.float32),
        "mem": n((N, U)).astype(np.float32),
        "offs": striped(np.random.permutation(T)[:S]),
        "n1": striped8(np.stack([np.random.permutation(S) for _ in range(8)])),
        "n2": striped8(np.stack([np.random.permutation(S) for _ in range(8)])),
        "n3": striped8(np.stack([np.random.permutation(S) for _ in range(8)])),
        "n4": striped8(np.stack([np.random.permutation(U)[:S] for _ in range(8)])),
        "n5": striped8(np.stack([np.random.permutation(U) for _ in range(8)])),
    }


def reference(x_words, x_scales, w1, gn, w2, mem, offs, n1, n2, n3, n4, n5):
    xq = unpack_weight(x_words, x_scales)[:, unstriped(offs)]
    y = mxq(f64(w1), 0, "e4m3").T @ xq
    pa = y[np.arange(H)[:, None], runs(n1, H)]
    z = f64(gn) * (pa + (sigmoid(y[np.arange(H)[:, None], runs(n2, H)])) * (y[np.arange(H)[:, None], runs(n3, H)] - pa))
    h = mxq(f64(w2), 0, "e4m3").T @ mxq(z, 0, "e4m3")
    pg = f64(mem).copy()
    pg[np.arange(N)[:, None], runs(n4, N)] = h
    return pg - (0.5 * (pg[np.arange(N)[:, None], runs(n5, N)]))

@@ -1,0 +1,192 @@
+from contextlib import ExitStack
+
+import concourse.mybir as mybir
+
+K, T, S, N, H, U = 512, 2048, 512, 512, 512, 1024
+FLOPS = 2 * K * H * S + 2 * H * N * S
+
+F32 = mybir.dt.float32
+BF16 = mybir.dt.bfloat16
+I32 = mybir.dt.int32
+U32 = mybir.dt.uint32
+U16 = mybir.dt.uint16
+U8 = mybir.dt.uint8
+FP8X4 = mybir.dt.float8_e4m3fn_x4
+ACT = mybir.ActivationFunctionType
+ALU = mybir.AluOpType
+
+P = 128
+PACK = 4
+HALF = S // 2
+LCOL = 16
+
+
+def tile_picked_laylerppagem_none_p_kernel(tc, x_words, x_scales, w1, gn, w2, mem, offs, n1, n2, n3, n4, n5, out):
+    nc = tc.nc
+    with ExitStack() as ctx:
+        keep = ctx.enter_context(tc.tile_pool(name="keep", bufs=1))
+        psum = ctx.enter_context(tc.psum_pool(name="psum", bufs=1))
+
+        def sb(name, shape, dtype):
+            return keep.tile(shape, dtype, name=name, align_bytes=64)
+
+        def load_list(name, src):
+            t = keep.tile(list(src.shape), U16, name=name, align_bytes=64)
+            nc.sync.dma_start(t[:], src)
+            return t
+
+        def entries(lst, first, count):
+            return lst[:, first // LCOL : (first + count) // LCOL]
+
+        xs_all = sb("xs_all", [P, T], U8)
+        nc.vector.memset(xs_all[:].bitcast(I32), 0)
+        warm_in = sb("warm_in", [P, 1], F32)
+        warm_out = sb("warm_out", [P, 1], F32)
+        nc.gpsimd.memset(warm_in[:], 0.0)
+        nc.scalar.activation(warm_out[:], warm_in[:], ACT.Sigmoid)
+
+        w1_raw = sb("w1_raw", [P, PACK, H], F32)
+        nc.sync.dma_start(w1_raw[:], w1.rearrange("(p j) c -> p j c", j=PACK))
+        for q in range(4):
+            nc.sync.dma_start(xs_all[32 * q : 32 * q + 4, :].bitcast(I32), x_scales[0, 4 * q : 4 * q + 4, :].bitcast(I32))
+        offs_sb = load_list("offs_sb", offs)
+        xw_all = sb("xw_all", [P, T], U32)
+        nc.sync.dma_start(xw_all[:].bitcast(I32), x_words[0].rearrange("p c r -> p (c r)").bitcast(I32))
+        n2_sb = load_list("n2_sb", n2)
+        gn_sb = sb("gn_sb", [P, PACK], F32)
+        nc.sync.dma_start(gn_sb[:], gn.rearrange("(p t) one -> p (t one)", t=PACK))
+        n3_sb = load_list("n3_sb", n3)
+        n1_sb = load_list("n1_sb", n1)
+        w2_raw = sb("w2_raw", [P, PACK, N], F32)
+        nc.sync.dma_start(w2_raw[:], w2.rearrange("(p j) c -> p j c", j=PACK))
+        n4_sb = load_list("n4_sb", n4)
+        n5_sb = load_list("n5_sb", n5)
+        mem_v = mem.rearrange("(p t) w -> p t w", t=PACK)
+        out_v = out.rearrange("(p t) w -> p t w", t=PACK)
+        page = []
+        for t in range(PACK):
+            pg = sb("page%d" % t, [P, U], F32)
+            nc.sync.dma_start(pg[:], mem_v[:, t, :])
+            page.append(pg)
+
+        def weight_tiles(name):
+            grouped = [sb("%s_bf%d" % (name, u), [P, 2, P, PACK], BF16) for u in range(2)]
+            codes = [sb("%s_codes%d" % (name, t), [P, P], U32) for t in range(PACK)]
+            scales = [sb("%s_scales%d" % (name, t), [P, P], U8) for t in range(PACK)]
+            return grouped, codes, scales
+
+        def deal(copy, raw, grouped, u):
+            src = raw[:].rearrange("p j (m t) -> p m t j", t=PACK)[:, :, 2 * u : 2 * u + 2, :]
+            copy(grouped[u][:].rearrange("p t m j -> p m t j"), src)
+
+        def quant_w(grouped, codes, scales, t):
+            nc.vector.quantize_mx(
+                out=codes[t][:].bitcast(FP8X4),
+                scales=scales[t][:],
+                in_=grouped[t // 2][:, t % 2].rearrange("p m j -> p (m j)"),
+            )
+
+        w1_bf, w1_codes, w1_scales = weight_tiles("w1")
+        w2_bf, w2_codes, w2_scales = weight_tiles("w2")
+        deal(nc.vector.tensor_copy, w1_raw, w1_bf, 0)
+        deal(nc.scalar.copy, w1_raw, w1_bf, 1)
+        quant_w(w1_bf, w1_codes, w1_scales, 0)
+        quant_w(w1_bf, w1_codes, w1_scales, 1)
+        xs = sb("xs", [P, S], U8)
+        nc.vector.tensor_copy(xs[:], xs_all[:].indirect(offs_sb[:]))
+        xw = [sb("xw%d" % c, [P, HALF], U32) for c in range(2)]
+        for c in range(2):
+            nc.vector.tensor_copy(xw[c][:], xw_all[:].indirect(entries(offs_sb, c * HALF, HALF)))
+        quant_w(w1_bf, w1_codes, w1_scales, 2)
+        quant_w(w1_bf, w1_codes, w1_scales, 3)
+
+        y = [sb("y%d" % t, [P, S], F32) for t in range(PACK)]
+
+        def first_product(t):
+            for c in range(2):
+                cols = slice(c * HALF, (c + 1) * HALF)
+                acc = psum.tile([P, HALF], F32, name="y_ps", tag="bank%d" % (2 * t + c))
+                nc.tensor.matmul_mx(
+                    out=acc[:], lhsT=w1_codes[t][:].bitcast(FP8X4), lhsT_scale=w1_scales[t][:],
+                    rhs=xw[c][:].bitcast(FP8X4), rhs_scale=xs[:, cols], start=True, stop=True,
+                )
+                (nc.scalar.copy, nc.vector.tensor_copy)[c](y[t][:, cols], acc[:])
+
+        part_a = [sb("part_a%d" % c, [P, PACK, HALF], F32) for c in range(2)]
+        part_b = [sb("part_b%d" % c, [P, PACK, HALF], F32) for c in range(2)]
+
+        def lerp(t, c):
+            s = sb("s%d_%d" % (t, c), [P, HALF], F32)
+            sg = sb("sg%d_%d" % (t, c), [P, HALF], F32)
+            sc = sb("sc%d_%d" % (t, c), [P, HALF], F32)
+            g = gn_sb[:, t : t + 1]
+            nc.scalar.activation(s[:], y[t][:].indirect(entries(n2_sb, c * HALF, HALF)), ACT.Sigmoid)
+            nc.scalar.activation(sg[:], s[:], ACT.Copy, scale=g)
+            nc.scalar.activation(sc[:], sg[:], ACT.Identity, bias=g, scale=-1.0)
+            nc.vector.tensor_tensor(part_b[c][:, t, :], y[t][:].indirect(entries(n3_sb, c * HALF, HALF)), sg[:], ALU.mult)
+            nc.vector.tensor_tensor(part_a[c][:, t, :], y[t][:].indirect(entries(n1_sb, c * HALF, HALF)), sc[:], ALU.mult)
+
+        h = {}
+
+        def second_product(c):
+            z_bf = sb("z_bf%d" % c, [P, HALF, PACK], BF16)
+            nc.vector.tensor_tensor(
+                z_bf[:].rearrange("p (c i) t -> p c t i", i=4),
+                part_a[c][:].rearrange("p t (c i) -> p c t i", i=4),
+                part_b[c][:].rearrange("p t (c i) -> p c t i", i=4),
+                ALU.add,
+            )
+            z_codes = sb("z_codes%d" % c, [P, HALF], U32)
+            z_scales = sb("z_scales%d" % c, [P, HALF], U8)
+            nc.vector.quantize_mx(out=z_codes[:].bitcast(FP8X4), scales=z_scales[:], in_=z_bf[:].rearrange("p c t -> p (c t)"))
+            for t in range(PACK):
+                acc = psum.tile([P, HALF], F32, name="h_ps", tag="bank%d" % (2 * t + c))
+                nc.tensor.matmul_mx(
+                    out=acc[:], lhsT=w2_codes[t][:].bitcast(FP8X4), lhsT_scale=w2_scales[t][:],
+                    rhs=z_codes[:].bitcast(FP8X4), rhs_scale=z_scales[:], start=True, stop=True,
+                )
+                h[t, c] = sb("h%d_%d" % (t, c), [P, HALF], F32)
+                nc.scalar.copy(h[t, c][:], acc[:])
+
+        def scatter(t, c):
+            nc.vector.tensor_copy(page[t][:].indirect(entries(n4_sb, c * HALF, HALF)), h[t, c][:])
+
+        first_product(0)
+        first_product(1)
+        lerp(0, 0)
+        deal(nc.vector.tensor_copy, w2_raw, w2_bf, 0)
+        first_product(2)
+        lerp(1, 0)
+        first_product(3)
+        lerp(2, 0)
+        deal(nc.scalar.copy, w2_raw, w2_bf, 1)
+        lerp(3, 0)
+        for t in range(PACK):
+            quant_w(w2_bf, w2_codes, w2_scales, t)
+        second_product(0)
+        lerp(0, 1)
+        for t in range(PACK - 1):
+            scatter(t, 0)
+            lerp(t + 1, 1)
+        second_product(1)
+        scatter(PACK - 1, 0)
+
+        def finish(t, pieces):
+            first = 0
+            for count in pieces:
+                res = sb("res%d_%d" % (t, first), [P, count], F32)
+                nc.vector.tensor_tensor(
+                    res[:], halfneg[t][:].indirect(entries(n5_sb, first, count)), page[t][:, first : first + count], ALU.add
+                )
+                nc.sync.dma_start(out_v[:, t, first : first + count], res[:])
+                first += count
+
+        halfneg = []
+        for t in range(PACK):
+            scatter(t, 1)
+            hn = sb("halfneg%d" % t, [P, U], F32)
+            nc.scalar.activation(hn[:], page[t][:], ACT.Copy, scale=-0.5)
+            halfneg.append(hn)
+            if t > 0:
+                finish(t - 1, (512, 512))
+        finish(PACK - 1, (512, 256, 256))

@@ -1,6 +1,7 @@
 from contextlib import ExitStack
 
 import concourse.mybir as mybir
+from concourse.masks import make_identity
 
 K, T, S, N, H, U = 512, 2048, 512, 512, 512, 1024
 FLOPS = 2 * K * H * S + 2 * H * N * S
@@ -27,8 +28,8 @@ def tile_picked_laylerppagem_none_p_kernel(tc, x_words, x_scales, w1, gn, w2, me
         keep = ctx.enter_context(tc.tile_pool(name="keep", bufs=1))
         psum = ctx.enter_context(tc.psum_pool(name="psum", bufs=1))
 
-        def sb(name, shape, dtype):
-            return keep.tile(shape, dtype, name=name, align_bytes=64)
+        def sb(name, shape, dtype, tag=None):
+            return keep.tile(shape, dtype, name=name, tag=tag or name, align_bytes=64)
 
         def load_list(name, src):
             t = keep.tile(list(src.shape), U16, name=name, align_bytes=64)
@@ -44,6 +45,9 @@ def tile_picked_laylerppagem_none_p_kernel(tc, x_words, x_scales, w1, gn, w2, me
         warm_out = sb("warm_out", [P, 1], F32)
         nc.gpsimd.memset(warm_in[:], 0.0)
         nc.scalar.activation(warm_out[:], warm_in[:], ACT.Sigmoid)
+
+        ident = sb("ident", [P, P], F32)
+        make_identity(nc, ident[:])
 
         w1_raw = sb("w1_raw", [P, PACK, H], F32)
         nc.sync.dma_start(w1_raw[:], w1.rearrange("(p j) c -> p j c", j=PACK))
@@ -126,27 +130,54 @@ def tile_picked_laylerppagem_none_p_kernel(tc, x_words, x_scales, w1, gn, w2, me
             nc.vector.tensor_tensor(part_b[c][:, t, :], y[t][:].indirect(entries(n3_sb, c * HALF, HALF)), sg[:], ALU.mult)
             nc.vector.tensor_tensor(part_a[c][:, t, :], y[t][:].indirect(entries(n1_sb, c * HALF, HALF)), sc[:], ALU.mult)
 
+        h_ps = {}
         h = {}
+        z_bf = [sb("z_bf%d" % c, [P, HALF, PACK], BF16) for c in range(2)]
 
-        def second_product(c):
-            z_bf = sb("z_bf%d" % c, [P, HALF, PACK], BF16)
+        def add_on_vector(c):
             nc.vector.tensor_tensor(
-                z_bf[:].rearrange("p (c i) t -> p c t i", i=4),
+                z_bf[c][:].rearrange("p (c i) t -> p c t i", i=4),
                 part_a[c][:].rearrange("p t (c i) -> p c t i", i=4),
                 part_b[c][:].rearrange("p t (c i) -> p c t i", i=4),
                 ALU.add,
             )
+
+        def add_on_tensor(c):
+            blocks = range(HALF // P)
+            zt_ps = [psum.tile([P, PACK, P], F32, name="zt_ps", tag="bank%d" % (2 * b + c)) for b in blocks]
+            for t in range(PACK):
+                for b in blocks:
+                    tok = slice(b * P, (b + 1) * P)
+                    nc.tensor.matmul(zt_ps[b][:, t, :], part_b[c][:, t, tok], ident[:], start=True, stop=False, is_transpose=True)
+                    nc.tensor.matmul(zt_ps[b][:, t, :], part_a[c][:, t, tok], ident[:], start=False, stop=True, is_transpose=True)
+            zt_bf = [sb("zt_bf%d" % b, [P, H], BF16) for b in blocks]
+            zw_ps = [psum.tile([P, 2, P], F32, name="zw_ps", tag="bank%d" % (4 + 2 * b + c)) for b in blocks]
+            for b in blocks:
+                nc.scalar.copy(
+                    zt_bf[b][:].rearrange("k (u p e) -> k u p e", u=2, e=2),
+                    zt_ps[b][:].rearrange("k (u e) p -> k u p e", e=2),
+                )
+                words = zt_bf[b][:].bitcast(F32)
+                for u in range(2):
+                    nc.tensor.transpose(zw_ps[b][:, u, :], words[:, u * P : (u + 1) * P], ident[:])
+            z_words = z_bf[c][:].bitcast(F32)
+            for b in blocks:
+                nc.scalar.copy(z_words[:, b * P : (b + 1) * P, :], zw_ps[b][:].rearrange("p u k -> p k u"))
+
+        def second_product(c):
             z_codes = sb("z_codes%d" % c, [P, HALF], U32)
             z_scales = sb("z_scales%d" % c, [P, HALF], U8)
-            nc.vector.quantize_mx(out=z_codes[:].bitcast(FP8X4), scales=z_scales[:], in_=z_bf[:].rearrange("p c t -> p (c t)"))
+            nc.vector.quantize_mx(out=z_codes[:].bitcast(FP8X4), scales=z_scales[:], in_=z_bf[c][:].rearrange("p c t -> p (c t)"))
             for t in range(PACK):
-                acc = psum.tile([P, HALF], F32, name="h_ps", tag="bank%d" % (2 * t + c))
+                h_ps[t, c] = psum.tile([P, HALF], F32, name="h_ps", tag="bank%d" % (2 * t + c))
                 nc.tensor.matmul_mx(
-                    out=acc[:], lhsT=w2_codes[t][:].bitcast(FP8X4), lhsT_scale=w2_scales[t][:],
+                    out=h_ps[t, c][:], lhsT=w2_codes[t][:].bitcast(FP8X4), lhsT_scale=w2_scales[t][:],
                     rhs=z_codes[:].bitcast(FP8X4), rhs_scale=z_scales[:], start=True, stop=True,
                 )
-                h[t, c] = sb("h%d_%d" % (t, c), [P, HALF], F32)
-                nc.scalar.copy(h[t, c][:], acc[:])
+
+        def copy_h(t, c, tag=None):
+            h[t, c] = sb("h%d_%d" % (t, c), [P, HALF], F32, tag=tag)
+            nc.scalar.copy(h[t, c][:], h_ps[t, c][:])
 
         def scatter(t, c):
             nc.vector.tensor_copy(page[t][:].indirect(entries(n4_sb, c * HALF, HALF)), h[t, c][:])
@@ -155,21 +186,27 @@ def tile_picked_laylerppagem_none_p_kernel(tc, x_words, x_scales, w1, gn, w2, me
         first_product(1)
         lerp(0, 0)
         deal(nc.vector.tensor_copy, w2_raw, w2_bf, 0)
+        deal(nc.vector.tensor_copy, w2_raw, w2_bf, 1)
         first_product(2)
         lerp(1, 0)
         first_product(3)
         lerp(2, 0)
-        deal(nc.scalar.copy, w2_raw, w2_bf, 1)
         lerp(3, 0)
         for t in range(PACK):
             quant_w(w2_bf, w2_codes, w2_scales, t)
+        add_on_vector(0)
         second_product(0)
-        lerp(0, 1)
-        for t in range(PACK - 1):
+        for t in range(PACK):
+            lerp(t, 1)
+        for t in (0, 1, 2):
+            copy_h(t, 0)
             scatter(t, 0)
-            lerp(t + 1, 1)
+        add_on_tensor(1)
         second_product(1)
-        scatter(PACK - 1, 0)
+        copy_h(3, 0, tag="zt_bf1")
+        scatter(3, 0)
+        for t in range(PACK):
+            copy_h(t, 1)
 
         def finish(t, pieces):
             first = 0

@@ -31,8 +31,11 @@ def tile_picked_laylerppagem_none_p_kernel(tc, x_words, x_scales, w1, gn, w2, me
         def sb(name, shape, dtype, tag=None):
             return keep.tile(shape, dtype, name=name, tag=tag or name, align_bytes=64)
 
+        def bank(b, shape):
+            return psum.tile(shape, F32, name="bank", tag="bank%d" % b)
+
         def load_list(name, src):
-            t = keep.tile(list(src.shape), U16, name=name, align_bytes=64)
+            t = sb(name, list(src.shape), U16)
             nc.sync.dma_start(t[:], src)
             return t
 
@@ -45,15 +48,16 @@ def tile_picked_laylerppagem_none_p_kernel(tc, x_words, x_scales, w1, gn, w2, me
         warm_out = sb("warm_out", [P, 1], F32)
         nc.gpsimd.memset(warm_in[:], 0.0)
         nc.scalar.activation(warm_out[:], warm_in[:], ACT.Sigmoid)
-
         ident = sb("ident", [P, P], F32)
         make_identity(nc, ident[:])
 
         w1_raw = sb("w1_raw", [P, PACK, H], F32)
-        nc.sync.dma_start(w1_raw[:], w1.rearrange("(p j) c -> p j c", j=PACK))
+        w1_v = w1.rearrange("(p j) c -> p j c", j=PACK)
+        nc.sync.dma_start(w1_raw[:, 0:2, :], w1_v[:, 0:2, :])
         for q in range(4):
             nc.sync.dma_start(xs_all[32 * q : 32 * q + 4, :].bitcast(I32), x_scales[0, 4 * q : 4 * q + 4, :].bitcast(I32))
         offs_sb = load_list("offs_sb", offs)
+        nc.sync.dma_start(w1_raw[:, 2:4, :], w1_v[:, 2:4, :])
         xw_all = sb("xw_all", [P, T], U32)
         nc.sync.dma_start(xw_all[:].bitcast(I32), x_words[0].rearrange("p c r -> p (c r)").bitcast(I32))
         n2_sb = load_list("n2_sb", n2)
@@ -67,91 +71,75 @@ def tile_picked_laylerppagem_none_p_kernel(tc, x_words, x_scales, w1, gn, w2, me
         n5_sb = load_list("n5_sb", n5)
         mem_v = mem.rearrange("(p t) w -> p t w", t=PACK)
         out_v = out.rearrange("(p t) w -> p t w", t=PACK)
-        page = []
+        page = [sb("page%d" % t, [P, U], F32) for t in range(PACK)]
         for t in range(PACK):
-            pg = sb("page%d" % t, [P, U], F32)
-            nc.sync.dma_start(pg[:], mem_v[:, t, :])
-            page.append(pg)
+            nc.sync.dma_start(page[t][:], mem_v[:, t, :])
 
-        def weight_tiles(name):
-            grouped = [sb("%s_bf%d" % (name, u), [P, 2, P, PACK], BF16) for u in range(2)]
-            codes = [sb("%s_codes%d" % (name, t), [P, P], U32) for t in range(PACK)]
-            scales = [sb("%s_scales%d" % (name, t), [P, P], U8) for t in range(PACK)]
-            return grouped, codes, scales
+        def quantise_weight(name, raw, first, count, copy):
+            grouped = sb("%s_bf%d" % (name, first), [P, count, P, PACK], BF16)
+            src = raw[:].rearrange("p j (m t) -> p m j t", t=PACK)[:, :, :, first : first + count]
+            copy(grouped[:].rearrange("p t m j -> p m j t"), src)
+            codes = sb("%s_codes%d" % (name, first), [P, count * P], U32)
+            scales = sb("%s_scales%d" % (name, first), [P, count * P], U8)
+            nc.vector.quantize_mx(out=codes[:].bitcast(FP8X4), scales=scales[:], in_=grouped[:].rearrange("p t m j -> p (t m j)"))
+            return {first + i: (codes[:, i * P : (i + 1) * P], scales[:, i * P : (i + 1) * P]) for i in range(count)}
 
-        def deal(copy, raw, grouped, u):
-            src = raw[:].rearrange("p j (m t) -> p m t j", t=PACK)[:, :, 2 * u : 2 * u + 2, :]
-            copy(grouped[u][:].rearrange("p t m j -> p m t j"), src)
-
-        def quant_w(grouped, codes, scales, t):
-            nc.vector.quantize_mx(
-                out=codes[t][:].bitcast(FP8X4),
-                scales=scales[t][:],
-                in_=grouped[t // 2][:, t % 2].rearrange("p m j -> p (m j)"),
+        def product(acc, weight, codes, scales):
+            nc.tensor.matmul_mx(
+                out=acc, lhsT=weight[0].bitcast(FP8X4), lhsT_scale=weight[1],
+                rhs=codes.bitcast(FP8X4), rhs_scale=scales, start=True, stop=True,
             )
 
-        w1_bf, w1_codes, w1_scales = weight_tiles("w1")
-        w2_bf, w2_codes, w2_scales = weight_tiles("w2")
-        deal(nc.vector.tensor_copy, w1_raw, w1_bf, 0)
-        deal(nc.scalar.copy, w1_raw, w1_bf, 1)
-        quant_w(w1_bf, w1_codes, w1_scales, 0)
-        quant_w(w1_bf, w1_codes, w1_scales, 1)
         xs = sb("xs", [P, S], U8)
         nc.vector.tensor_copy(xs[:], xs_all[:].indirect(offs_sb[:]))
+        w1_q = quantise_weight("w1", w1_raw, 0, 2, nc.vector.tensor_copy)
+        w1_q.update(quantise_weight("w1", w1_raw, 2, 2, nc.scalar.copy))
         xw = [sb("xw%d" % c, [P, HALF], U32) for c in range(2)]
         for c in range(2):
             nc.vector.tensor_copy(xw[c][:], xw_all[:].indirect(entries(offs_sb, c * HALF, HALF)))
-        quant_w(w1_bf, w1_codes, w1_scales, 2)
-        quant_w(w1_bf, w1_codes, w1_scales, 3)
 
         y = [sb("y%d" % t, [P, S], F32) for t in range(PACK)]
+        yg = [sb("yg%d" % t, [P, S], F32) for t in range(PACK)]
 
-        def first_product(t):
-            for c in range(2):
-                cols = slice(c * HALF, (c + 1) * HALF)
-                acc = psum.tile([P, HALF], F32, name="y_ps", tag="bank%d" % (2 * t + c))
-                nc.tensor.matmul_mx(
-                    out=acc[:], lhsT=w1_codes[t][:].bitcast(FP8X4), lhsT_scale=w1_scales[t][:],
-                    rhs=xw[c][:].bitcast(FP8X4), rhs_scale=xs[:, cols], start=True, stop=True,
-                )
-                (nc.scalar.copy, nc.vector.tensor_copy)[c](y[t][:, cols], acc[:])
+        def first_product(t, b, halves, copy):
+            acc = bank(b, [P, len(halves) * HALF])
+            for i, c in enumerate(halves):
+                product(acc[:, i * HALF : (i + 1) * HALF], w1_q[t], xw[c][:], xs[:, c * HALF : (c + 1) * HALF])
+            copy(y[t][:, halves[0] * HALF : (halves[-1] + 1) * HALF], acc[:])
+
+        def gain(t):
+            nc.vector.tensor_scalar(yg[t][:], y[t][:], gn_sb[:, t : t + 1], None, ALU.mult)
 
         part_a = [sb("part_a%d" % c, [P, PACK, HALF], F32) for c in range(2)]
         part_b = [sb("part_b%d" % c, [P, PACK, HALF], F32) for c in range(2)]
 
         def lerp(t, c):
             s = sb("s%d_%d" % (t, c), [P, HALF], F32)
-            sg = sb("sg%d_%d" % (t, c), [P, HALF], F32)
-            sc = sb("sc%d_%d" % (t, c), [P, HALF], F32)
-            g = gn_sb[:, t : t + 1]
+            rest = sb("rest%d_%d" % (t, c), [P, HALF], F32)
             nc.scalar.activation(s[:], y[t][:].indirect(entries(n2_sb, c * HALF, HALF)), ACT.Sigmoid)
-            nc.scalar.activation(sg[:], s[:], ACT.Copy, scale=g)
-            nc.scalar.activation(sc[:], sg[:], ACT.Identity, bias=g, scale=-1.0)
-            nc.vector.tensor_tensor(part_b[c][:, t, :], y[t][:].indirect(entries(n3_sb, c * HALF, HALF)), sg[:], ALU.mult)
-            nc.vector.tensor_tensor(part_a[c][:, t, :], y[t][:].indirect(entries(n1_sb, c * HALF, HALF)), sc[:], ALU.mult)
+            nc.scalar.activation(rest[:], s[:], ACT.Copy, bias=1.0, scale=-1.0)
+            nc.vector.tensor_tensor(part_b[c][:, t, :], yg[t][:].indirect(entries(n3_sb, c * HALF, HALF)), s[:], ALU.mult)
+            nc.vector.tensor_tensor(part_a[c][:, t, :], yg[t][:].indirect(entries(n1_sb, c * HALF, HALF)), rest[:], ALU.mult)
 
-        h_ps = {}
-        h = {}
         z_bf = [sb("z_bf%d" % c, [P, HALF, PACK], BF16) for c in range(2)]
 
-        def add_on_vector(c):
+        def add_on_vector(c, tok):
             nc.vector.tensor_tensor(
-                z_bf[c][:].rearrange("p (c i) t -> p c t i", i=4),
-                part_a[c][:].rearrange("p t (c i) -> p c t i", i=4),
-                part_b[c][:].rearrange("p t (c i) -> p c t i", i=4),
+                z_bf[c][:, tok, :].rearrange("p (c i) t -> p c t i", i=4),
+                part_a[c][:, :, tok].rearrange("p t (c i) -> p c t i", i=4),
+                part_b[c][:, :, tok].rearrange("p t (c i) -> p c t i", i=4),
                 ALU.add,
             )
 
-        def add_on_tensor(c):
-            blocks = range(HALF // P)
-            zt_ps = [psum.tile([P, PACK, P], F32, name="zt_ps", tag="bank%d" % (2 * b + c)) for b in blocks]
+        def add_on_tensor(c, blocks, sum_banks, back_banks):
+            zt_ps = {b: bank(sum_banks[b], [P, PACK, P]) for b in blocks}
             for t in range(PACK):
                 for b in blocks:
                     tok = slice(b * P, (b + 1) * P)
                     nc.tensor.matmul(zt_ps[b][:, t, :], part_b[c][:, t, tok], ident[:], start=True, stop=False, is_transpose=True)
                     nc.tensor.matmul(zt_ps[b][:, t, :], part_a[c][:, t, tok], ident[:], start=False, stop=True, is_transpose=True)
-            zt_bf = [sb("zt_bf%d" % b, [P, H], BF16) for b in blocks]
-            zw_ps = [psum.tile([P, 2, P], F32, name="zw_ps", tag="bank%d" % (4 + 2 * b + c)) for b in blocks]
+            zt_bf = {b: sb("zt_bf%d_%d" % (c, b), [P, H], BF16) for b in blocks}
+            zw_ps = {b: bank(back_banks[b], [P, 2, P]) for b in blocks}
             for b in blocks:
                 nc.scalar.copy(
                     zt_bf[b][:].rearrange("k (u p e) -> k u p e", u=2, e=2),
@@ -164,49 +152,52 @@ def tile_picked_laylerppagem_none_p_kernel(tc, x_words, x_scales, w1, gn, w2, me
             for b in blocks:
                 nc.scalar.copy(z_words[:, b * P : (b + 1) * P, :], zw_ps[b][:].rearrange("p u k -> p k u"))
 
-        def second_product(c):
-            z_codes = sb("z_codes%d" % c, [P, HALF], U32)
-            z_scales = sb("z_scales%d" % c, [P, HALF], U8)
-            nc.vector.quantize_mx(out=z_codes[:].bitcast(FP8X4), scales=z_scales[:], in_=z_bf[c][:].rearrange("p c t -> p (c t)"))
-            for t in range(PACK):
-                h_ps[t, c] = psum.tile([P, HALF], F32, name="h_ps", tag="bank%d" % (2 * t + c))
-                nc.tensor.matmul_mx(
-                    out=h_ps[t, c][:], lhsT=w2_codes[t][:].bitcast(FP8X4), lhsT_scale=w2_scales[t][:],
-                    rhs=z_codes[:].bitcast(FP8X4), rhs_scale=z_scales[:], start=True, stop=True,
-                )
+        def quantise_z(c):
+            codes = sb("z_codes%d" % c, [P, HALF], U32)
+            scales = sb("z_scales%d" % c, [P, HALF], U8)
+            nc.vector.quantize_mx(out=codes[:].bitcast(FP8X4), scales=scales[:], in_=z_bf[c][:].rearrange("p c t -> p (c t)"))
+            return codes, scales
 
-        def copy_h(t, c, tag=None):
-            h[t, c] = sb("h%d_%d" % (t, c), [P, HALF], F32, tag=tag)
-            nc.scalar.copy(h[t, c][:], h_ps[t, c][:])
+        def second_product(t, b, z_q):
+            acc = bank(b, [P, HALF])
+            product(acc[:], w2_q[t], z_q[0][:], z_q[1][:])
+            return acc
 
-        def scatter(t, c):
-            nc.vector.tensor_copy(page[t][:].indirect(entries(n4_sb, c * HALF, HALF)), h[t, c][:])
+        def put(t, c, acc, tag=None):
+            h = sb("h%d_%d" % (t, c), [P, HALF], F32, tag=tag)
+            nc.scalar.copy(h[:], acc[:])
+            nc.vector.tensor_copy(page[t][:].indirect(entries(n4_sb, c * HALF, HALF)), h[:])
 
-        first_product(0)
-        first_product(1)
+        lo, hi, both = (0,), (1,), (0, 1)
+        first_product(0, 0, lo, nc.scalar.copy)
+        first_product(1, 1, lo, nc.scalar.copy)
+        first_product(0, 2, hi, nc.vector.tensor_copy)
+        first_product(1, 3, hi, nc.vector.tensor_copy)
+        gain(0)
         lerp(0, 0)
-        deal(nc.vector.tensor_copy, w2_raw, w2_bf, 0)
-        deal(nc.vector.tensor_copy, w2_raw, w2_bf, 1)
-        first_product(2)
+        gain(1)
         lerp(1, 0)
-        first_product(3)
-        lerp(2, 0)
-        lerp(3, 0)
-        for t in range(PACK):
-            quant_w(w2_bf, w2_codes, w2_scales, t)
-        add_on_vector(0)
-        second_product(0)
-        for t in range(PACK):
-            lerp(t, 1)
-        for t in (0, 1, 2):
-            copy_h(t, 0)
-            scatter(t, 0)
-        add_on_tensor(1)
-        second_product(1)
-        copy_h(3, 0, tag="zt_bf1")
-        scatter(3, 0)
-        for t in range(PACK):
-            copy_h(t, 1)
+        for t in (2, 3):
+            first_product(t, 2 + t, both, nc.scalar.copy)
+            gain(t)
+            lerp(t, 0)
+        add_on_vector(0, slice(0, P))
+        lerp(0, 1)
+        w2_q = quantise_weight("w2", w2_raw, 0, 2, nc.scalar.copy)
+        lerp(1, 1)
+        add_on_tensor(0, (1,), (None, 6), (None, 7))
+        z0 = quantise_z(0)
+        lerp(2, 1)
+        lerp(3, 1)
+        put(0, 0, second_product(0, 0, z0))
+        w2_q.update(quantise_weight("w2", w2_raw, 2, 2, nc.scalar.copy))
+        put(1, 0, second_product(1, 1, z0))
+        put(2, 0, second_product(2, 2, z0))
+        last_acc = second_product(3, 3, z0)
+        add_on_tensor(1, (0, 1), (4, 5), (6, 7))
+        z1 = quantise_z(1)
+        accs = [second_product(t, (0, 1, 2, 4)[t], z1) for t in range(PACK)]
+        put(PACK - 1, 0, last_acc, tag="zt_bf1_1")
 
         def finish(t, pieces):
             first = 0
@@ -218,12 +209,9 @@ def tile_picked_laylerppagem_none_p_kernel(tc, x_words, x_scales, w1, gn, w2, me
                 nc.sync.dma_start(out_v[:, t, first : first + count], res[:])
                 first += count
 
-        halfneg = []
+        halfneg = [sb("halfneg%d" % t, [P, U], F32) for t in range(PACK)]
         for t in range(PACK):
-            scatter(t, 1)
-            hn = sb("halfneg%d" % t, [P, U], F32)
-            nc.scalar.activation(hn[:], page[t][:], ACT.Copy, scale=-0.5)
-            halfneg.append(hn)
-            if t > 0:
-                finish(t - 1, (512, 512))
-        finish(PACK - 1, (512, 256, 256))
+            put(t, 1, accs[t])
+        for t in range(PACK):
+            nc.scalar.activation(halfneg[t][:], page[t][:], ACT.Copy, scale=-0.5)
+            finish(t, (512, 512) if t < PACK - 1 else (512, 256, 256))

@@ -121,8 +121,6 @@ def tile_picked_laylerppagem_none_p_kernel(tc, x_words, x_scales, w1, gn, w2, me
             nc.vector.tensor_tensor(part_b[c][:, t, :], yg[t][:].indirect(entries(n3_sb, c * HALF, HALF)), s[:], ALU.mult)
             nc.vector.tensor_tensor(part_a[c][:, t, :], yg[t][:].indirect(entries(n1_sb, c * HALF, HALF)), rest[:], ALU.mult)
 
-        z_bf = [sb("z_bf%d" % c, [P, HALF, PACK], BF16) for c in range(2)]
-
         def add_on_vector(c, tok):
             nc.vector.tensor_tensor(
                 z_bf[c][:, tok, :].rearrange("p (c i) t -> p c t i", i=4),
@@ -171,7 +169,7 @@ def tile_picked_laylerppagem_none_p_kernel(tc, x_words, x_scales, w1, gn, w2, me
         lo, hi, both = (0,), (1,), (0, 1)
         first_product(0, 0, lo, nc.scalar.copy)
         first_product(1, 1, lo, nc.scalar.copy)
-        first_product(0, 2, hi, nc.vector.tensor_copy)
+        first_product(0, 2, hi, nc.scalar.copy)
         first_product(1, 3, hi, nc.vector.tensor_copy)
         gain(0)
         lerp(0, 0)
@@ -181,8 +179,9 @@ def tile_picked_laylerppagem_none_p_kernel(tc, x_words, x_scales, w1, gn, w2, me
             first_product(t, 2 + t, both, nc.scalar.copy)
             gain(t)
             lerp(t, 0)
-        add_on_vector(0, slice(0, P))
         lerp(0, 1)
+        z_bf = [sb("z_bf0", [P, HALF, PACK], BF16, tag="s0_1"), sb("z_bf1", [P, HALF, PACK], BF16)]
+        add_on_vector(0, slice(0, P))
         w2_q = quantise_weight("w2", w2_raw, 0, 2, nc.scalar.copy)
         lerp(1, 1)
         add_on_tensor(0, (1,), (None, 6), (None, 7))

from contextlib import ExitStack

import concourse.mybir as mybir
from concourse.masks import make_identity

K, T, S, N, H, U = 512, 2048, 512, 512, 512, 1024
FLOPS = 2 * K * H * S + 2 * H * N * S

F32 = mybir.dt.float32
BF16 = mybir.dt.bfloat16
I32 = mybir.dt.int32
U32 = mybir.dt.uint32
U16 = mybir.dt.uint16
U8 = mybir.dt.uint8
FP8X4 = mybir.dt.float8_e4m3fn_x4
ACT = mybir.ActivationFunctionType
ALU = mybir.AluOpType

P = 128
PACK = 4
HALF = S // 2
LCOL = 16


def tile_picked_laylerppagem_none_p_kernel(tc, x_words, x_scales, w1, gn, w2, mem, offs, n1, n2, n3, n4, n5, out):
    nc = tc.nc
    with ExitStack() as ctx:
        keep = ctx.enter_context(tc.tile_pool(name="keep", bufs=1))
        psum = ctx.enter_context(tc.psum_pool(name="psum", bufs=1))

        def sb(name, shape, dtype, tag=None):
            return keep.tile(shape, dtype, name=name, tag=tag or name, align_bytes=64)

        def bank(b, shape):
            return psum.tile(shape, F32, name="bank", tag="bank%d" % b)

        def load_list(name, src):
            t = sb(name, list(src.shape), U16)
            nc.sync.dma_start(t[:], src)
            return t

        def entries(lst, first, count):
            return lst[:, first // LCOL : (first + count) // LCOL]

        xs_all = sb("xs_all", [P, T], U8)
        nc.vector.memset(xs_all[:].bitcast(I32), 0)
        warm_in = sb("warm_in", [P, 1], F32)
        warm_out = sb("warm_out", [P, 1], F32)
        nc.gpsimd.memset(warm_in[:], 0.0)
        nc.scalar.activation(warm_out[:], warm_in[:], ACT.Sigmoid)
        ident = sb("ident", [P, P], F32)
        make_identity(nc, ident[:])

        w1_raw = sb("w1_raw", [P, PACK, H], F32)
        w1_v = w1.rearrange("(p j) c -> p j c", j=PACK)
        nc.sync.dma_start(w1_raw[:, 0:2, :], w1_v[:, 0:2, :])
        for q in range(4):
            nc.sync.dma_start(xs_all[32 * q : 32 * q + 4, :].bitcast(I32), x_scales[0, 4 * q : 4 * q + 4, :].bitcast(I32))
        offs_sb = load_list("offs_sb", offs)
        nc.sync.dma_start(w1_raw[:, 2:4, :], w1_v[:, 2:4, :])
        xw_all = sb("xw_all", [P, T], U32)
        nc.sync.dma_start(xw_all[:].bitcast(I32), x_words[0].rearrange("p c r -> p (c r)").bitcast(I32))
        n2_sb = load_list("n2_sb", n2)
        gn_sb = sb("gn_sb", [P, PACK], F32)
        nc.sync.dma_start(gn_sb[:], gn.rearrange("(p t) one -> p (t one)", t=PACK))
        n3_sb = load_list("n3_sb", n3)
        n1_sb = load_list("n1_sb", n1)
        w2_raw = sb("w2_raw", [P, PACK, N], F32)
        nc.sync.dma_start(w2_raw[:], w2.rearrange("(p j) c -> p j c", j=PACK))
        n4_sb = load_list("n4_sb", n4)
        n5_sb = load_list("n5_sb", n5)
        mem_v = mem.rearrange("(p t) w -> p t w", t=PACK)
        out_v = out.rearrange("(p t) w -> p t w", t=PACK)
        page = [sb("page%d" % t, [P, U], F32) for t in range(PACK)]
        for t in range(PACK):
            nc.sync.dma_start(page[t][:], mem_v[:, t, :])

        def quantise_weight(name, raw, first, count, copy):
            grouped = sb("%s_bf%d" % (name, first), [P, count, P, PACK], BF16)
            src = raw[:].rearrange("p j (m t) -> p m j t", t=PACK)[:, :, :, first : first + count]
            copy(grouped[:].rearrange("p t m j -> p m j t"), src)
            codes = sb("%s_codes%d" % (name, first), [P, count * P], U32)
            scales = sb("%s_scales%d" % (name, first), [P, count * P], U8)
            nc.vector.quantize_mx(out=codes[:].bitcast(FP8X4), scales=scales[:], in_=grouped[:].rearrange("p t m j -> p (t m j)"))
            return {first + i: (codes[:, i * P : (i + 1) * P], scales[:, i * P : (i + 1) * P]) for i in range(count)}

        def product(acc, weight, codes, scales):
            nc.tensor.matmul_mx(
                out=acc, lhsT=weight[0].bitcast(FP8X4), lhsT_scale=weight[1],
                rhs=codes.bitcast(FP8X4), rhs_scale=scales, start=True, stop=True,
            )

        xs = sb("xs", [P, S], U8)
        nc.vector.tensor_copy(xs[:], xs_all[:].indirect(offs_sb[:]))
        w1_q = quantise_weight("w1", w1_raw, 0, 2, nc.vector.tensor_copy)
        w1_q.update(quantise_weight("w1", w1_raw, 2, 2, nc.scalar.copy))
        xw = [sb("xw%d" % c, [P, HALF], U32) for c in range(2)]
        for c in range(2):
            nc.vector.tensor_copy(xw[c][:], xw_all[:].indirect(entries(offs_sb, c * HALF, HALF)))

        y = [sb("y%d" % t, [P, S], F32) for t in range(PACK)]
        yg = [sb("yg%d" % t, [P, S], F32) for t in range(PACK)]

        def first_product(t, b, halves, copy):
            acc = bank(b, [P, len(halves) * HALF])
            for i, c in enumerate(halves):
                product(acc[:, i * HALF : (i + 1) * HALF], w1_q[t], xw[c][:], xs[:, c * HALF : (c + 1) * HALF])
            copy(y[t][:, halves[0] * HALF : (halves[-1] + 1) * HALF], acc[:])

        def gain(t):
            nc.vector.tensor_scalar(yg[t][:], y[t][:], gn_sb[:, t : t + 1], None, ALU.mult)

        part_a = [sb("part_a%d" % c, [P, PACK, HALF], F32) for c in range(2)]
        part_b = [sb("part_b%d" % c, [P, PACK, HALF], F32) for c in range(2)]

        def lerp(t, c):
            s = sb("s%d_%d" % (t, c), [P, HALF], F32)
            rest = sb("rest%d_%d" % (t, c), [P, HALF], F32)
            nc.scalar.activation(s[:], y[t][:].indirect(entries(n2_sb, c * HALF, HALF)), ACT.Sigmoid)
            nc.scalar.activation(rest[:], s[:], ACT.Copy, bias=1.0, scale=-1.0)
            nc.vector.tensor_tensor(part_b[c][:, t, :], yg[t][:].indirect(entries(n3_sb, c * HALF, HALF)), s[:], ALU.mult)
            nc.vector.tensor_tensor(part_a[c][:, t, :], yg[t][:].indirect(entries(n1_sb, c * HALF, HALF)), rest[:], ALU.mult)

        def add_on_vector(c, tok):
            nc.vector.tensor_tensor(
                z_bf[c][:, tok, :].rearrange("p (c i) t -> p c t i", i=4),
                part_a[c][:, :, tok].rearrange("p t (c i) -> p c t i", i=4),
                part_b[c][:, :, tok].rearrange("p t (c i) -> p c t i", i=4),
                ALU.add,
            )

        def add_on_tensor(c, blocks, sum_banks, back_banks):
            zt_ps = {b: bank(sum_banks[b], [P, PACK, P]) for b in blocks}
            for t in range(PACK):
                for b in blocks:
                    tok = slice(b * P, (b + 1) * P)
                    nc.tensor.matmul(zt_ps[b][:, t, :], part_b[c][:, t, tok], ident[:], start=True, stop=False, is_transpose=True)
                    nc.tensor.matmul(zt_ps[b][:, t, :], part_a[c][:, t, tok], ident[:], start=False, stop=True, is_transpose=True)
            zt_bf = {b: sb("zt_bf%d_%d" % (c, b), [P, H], BF16) for b in blocks}
            zw_ps = {b: bank(back_banks[b], [P, 2, P]) for b in blocks}
            for b in blocks:
                nc.scalar.copy(
                    zt_bf[b][:].rearrange("k (u p e) -> k u p e", u=2, e=2),
                    zt_ps[b][:].rearrange("k (u e) p -> k u p e", e=2),
                )
                words = zt_bf[b][:].bitcast(F32)
                for u in range(2):
                    nc.tensor.transpose(zw_ps[b][:, u, :], words[:, u * P : (u + 1) * P], ident[:])
            z_words = z_bf[c][:].bitcast(F32)
            for b in blocks:
                nc.scalar.copy(z_words[:, b * P : (b + 1) * P, :], zw_ps[b][:].rearrange("p u k -> p k u"))

        def quantise_z(c):
            codes = sb("z_codes%d" % c, [P, HALF], U32)
            scales = sb("z_scales%d" % c, [P, HALF], U8)
            nc.vector.quantize_mx(out=codes[:].bitcast(FP8X4), scales=scales[:], in_=z_bf[c][:].rearrange("p c t -> p (c t)"))
            return codes, scales

        def second_product(t, b, z_q):
            acc = bank(b, [P, HALF])
            product(acc[:], w2_q[t], z_q[0][:], z_q[1][:])
            return acc

        def put(t, c, acc, tag=None):
            h = sb("h%d_%d" % (t, c), [P, HALF], F32, tag=tag)
            nc.scalar.copy(h[:], acc[:])
            nc.vector.tensor_copy(page[t][:].indirect(entries(n4_sb, c * HALF, HALF)), h[:])

        lo, hi, both = (0,), (1,), (0, 1)
        first_product(0, 0, lo, nc.scalar.copy)
        first_product(1, 1, lo, nc.scalar.copy)
        first_product(0, 2, hi, nc.scalar.copy)
        first_product(1, 3, hi, nc.vector.tensor_copy)
        gain(0)
        lerp(0, 0)
        gain(1)
        lerp(1, 0)
        for t in (2, 3):
            first_product(t, 2 + t, both, nc.scalar.copy)
            gain(t)
            lerp(t, 0)
        lerp(0, 1)
        z_bf = [sb("z_bf0", [P, HALF, PACK], BF16, tag="s0_1"), sb("z_bf1", [P, HALF, PACK], BF16)]
        add_on_vector(0, slice(0, P))
        w2_q = quantise_weight("w2", w2_raw, 0, 2, nc.scalar.copy)
        lerp(1, 1)
        add_on_tensor(0, (1,), (None, 6), (None, 7))
        z0 = quantise_z(0)
        lerp(2, 1)
        lerp(3, 1)
        put(0, 0, second_product(0, 0, z0))
        w2_q.update(quantise_weight("w2", w2_raw, 2, 2, nc.scalar.copy))
        put(1, 0, second_product(1, 1, z0))
        put(2, 0, second_product(2, 2, z0))
        last_acc = second_product(3, 3, z0)
        add_on_tensor(1, (0, 1), (4, 5), (6, 7))
        z1 = quantise_z(1)
        accs = [second_product(t, (0, 1, 2, 4)[t], z1) for t in range(PACK)]
        put(PACK - 1, 0, last_acc, tag="zt_bf1_1")

        def finish(t, pieces):
            first = 0
            for count in pieces:
                res = sb("res%d_%d" % (t, first), [P, count], F32)
                nc.vector.tensor_tensor(
                    res[:], halfneg[t][:].indirect(entries(n5_sb, first, count)), page[t][:, first : first + count], ALU.add
                )
                nc.sync.dma_start(out_v[:, t, first : first + count], res[:])
                first += count

        halfneg = [sb("halfneg%d" % t, [P, U], F32) for t in range(PACK)]
        for t in range(PACK):
            put(t, 1, accs[t])
        for t in range(PACK):
            nc.scalar.activation(halfneg[t][:], page[t][:], ACT.Copy, scale=-0.5)
            finish(t, (512, 512) if t < PACK - 1 else (512, 256, 256))
